import numpy as np
import ml_dtypes


def mxq(x, axis, fmt="e4m3"):
    dtype, down = {"e4m3": (ml_dtypes.float8_e4m3fn, 7), "e5m2": (ml_dtypes.float8_e5m2, 14)}[fmt]
    v = np.moveaxis(np.asarray(x, np.float32).astype(ml_dtypes.bfloat16).astype(np.float64), axis, -1)
    blocks = v.reshape(v.shape[:-1] + (-1, 32))
    amax = np.abs(blocks).max(-1, keepdims=True)
    byte = np.maximum(np.where(amax > 0, np.frexp(amax)[1] - 1 + 127, 0) - down, 1)
    scale = np.exp2(byte - 127.0)
    codes = (blocks / scale).astype(np.float32).astype(dtype).astype(np.float64)
    return np.moveaxis((codes * scale).reshape(v.shape), -1, axis)


WIDE = False


def mx_kscale(k, group=512):
    if not WIDE:
        return np.ones(k)
    levels = np.array([10, -10, 5, -5, 0])
    if group != 512:
        return np.exp2(np.random.permutation(np.resize(levels, k // group))).repeat(group)
    if k % 512:
        return np.exp2(np.random.permutation(np.resize(levels, k // 32))).repeat(32)
    a = np.empty((k // 512, 16))
    for p in range(k // 512):
        a[p, :8] = np.random.permutation(np.resize(levels, 8))
        for g in range(8):
            far = levels[np.abs(levels - a[p, g]) >= 10]
            a[p, g + 8] = far[np.random.randint(len(far))]
    return np.exp2(a.ravel()).repeat(32)


def f64(x):
    return np.asarray(x).astype(np.float64)


def striped(idx):
    return np.tile(np.asarray(idx).reshape(-1, 16).T, (8, 1)).astype(np.uint16)


def unstriped(offs):
    return offs[:16].T.reshape(-1).astype(np.int64)


H, KV, D, NQ, N = 8, 8, 128, 512, 512
CAP = 2.0


def setup_inputs():
    n = np.random.standard_normal
    s = mx_kscale(D, 0)[:, None]
    u = mx_kscale(N)
    t = np.random.uniform(0.5, 2.0, N) * u
    v = n((KV, N, 128))
    return {
        "qT": (n((H, D, NQ)) * s * (0.70 / np.sqrt(D))).astype(np.float32),
        "kT": (n((KV, D, N)) / s).astype(np.float32),
        "t": t.reshape(N, 1).astype(np.float32),
        "v": (v / t[:, None]).astype(np.float32),
        "kb": (0.5 * n((N, 1))).astype(np.float32),
    }


def reference(qT, kT, t, v, kb):
    a = mxq(f64(kT), 1, "e4m3").transpose(0, 2, 1) @ mxq(f64(qT), 1, "e4m3")
    a = a + f64(kb)
    a = CAP * np.tanh(a / CAP)
    p = np.maximum(a, 0.0)
    w = p * f64(t)
    y = mxq(w, 1, "e4m3").transpose(0, 2, 1) @ mxq(f64(v), 1, "e4m3")
    y = y / 16.0
    return y

@@ -1,0 +1,249 @@
+from contextlib import ExitStack
+
+import concourse.mybir as mybir
+
+H, D, NQ, N = 8, 128, 512, 512
+FLOPS = 2 * 2 * H * D * NQ * N
+
+F32 = mybir.dt.float32
+BF16 = mybir.dt.bfloat16
+U32 = mybir.dt.uint32
+U8 = mybir.dt.uint8
+FP8X4 = mybir.dt.float8_e4m3fn_x4
+ACT = mybir.ActivationFunctionType
+ALU = mybir.AluOpType
+
+P = 128
+PACK = 4
+ROWS = 32
+SETS = 2
+SKEW = 3
+HEAD_SPLIT = 40
+BANKS = (2, 1, 1, 2)
+PRODUCT_LAG = 5
+STORE_LAG = 1
+K1_STEP = 0
+Q1_STEP = 4
+V_LEAD = 0
+Q1_SPLIT = 48
+V_GAP = 2
+V_ON_SCALAR = 8
+SHARED_FROM = 7
+SHARE = 64
+CAP_BUFS = 12
+
+
+def tile_rows_a_relu_kb_cap_kernel(tc, qT, kT, t, v, kb, out):
+    nc = tc.nc
+    with ExitStack() as ctx:
+        keep = ctx.enter_context(tc.tile_pool(name="keep", bufs=1))
+        ring = ctx.enter_context(tc.tile_pool(name="ring", bufs=4))
+        psum = ctx.enter_context(tc.psum_pool(name="psum", bufs=1))
+        ctx.enter_context(tc.manual_schedule())
+
+        def kept(name, shape, dtype):
+            return keep.tile(shape, dtype, name=name, align_bytes=64)
+
+        kb_sb = kept("kb_sb", [P, PACK], F32)
+        t_sb = kept("t_sb", [P, PACK], F32)
+        half_kb = kept("half_kb", [P, PACK], F32)
+        warm = kept("warm", [P, PACK], F32)
+        raw = {}
+        packed = {}
+        codes = {}
+        scales = {}
+        for name in ("k", "q", "v"):
+            for s in range(SETS):
+                raw[name, s] = kept("raw_%s%d" % (name, s), [P, PACK, 512], F32)
+                packed[name, s] = kept("packed_%s%d" % (name, s), [P, 512, PACK], BF16)
+                codes[name, s] = kept("codes_%s%d" % (name, s), [P, 512], U32)
+                scales[name, s] = kept("scales_%s%d" % (name, s), [P, 512], U8)
+        score_banks = [
+            [psum.tile([P, NQ], F32, name="score_%d_%d" % (g, b)) for b in range(BANKS[g])] for g in range(PACK)
+        ]
+        out_banks = [psum.tile([P, NQ], F32, name="out_bank_%d" % b) for b in range(2)]
+
+        def load(name, s):
+            heads = slice(PACK * s, PACK * (s + 1))
+            if name == "v":
+                src = v[heads].rearrange("h (p r) e -> p h (r e)", r=PACK)
+            else:
+                src = (kT if name == "k" else qT)[heads].rearrange("h (p j) n -> (h p) j n", j=PACK)
+            nc.sync.dma_start(out=raw[name, s][:], in_=src)
+
+        def copy_on(engine, dst, src):
+            if engine == "vector":
+                nc.vector.tensor_copy(out=dst, in_=src)
+            else:
+                nc.scalar.copy(out=dst, in_=src)
+
+        def pack_dealt(name, s, engine, lo, hi):
+            dst = packed[name, s][:].rearrange("p (c a b) j -> p a j b c", c=PACK, b=2)
+            src = raw[name, s][:].rearrange("p j (a b c) -> p a j b c", c=PACK, b=2)
+            copy_on(engine, dst[:, lo:hi], src[:, lo:hi])
+
+        def pack_v(s, g, engine):
+            dst = packed["v", s][:, P * g : P * (g + 1), :].rearrange("p (a i) r -> p a r i", i=PACK)
+            src = raw["v", s][:, g, :].rearrange("p (r a i) -> p a r i", r=PACK, i=PACK)
+            copy_on(engine, dst, src)
+
+        def quantize(name, s, lo=0, hi=512):
+            nc.vector.quantize_mx(
+                out=codes[name, s][:, lo:hi].bitcast(FP8X4),
+                scales=scales[name, s][:, lo:hi],
+                in_=packed[name, s][:, lo:hi, :].rearrange("p n j -> p (n j)"),
+            )
+
+        order = [(h, r) for key, h, r in sorted((PACK * h + SKEW * r, h, r) for h in range(H) for r in range(PACK))]
+        steps = len(order)
+        done_at = {order.index((h, PACK - 1)): h for h in range(H)}
+
+        def bank_of(n):
+            h, r = order[n]
+            g = h % PACK
+            return g, r % BANKS[g]
+
+        def scores(n):
+            h, r = order[n]
+            s, g = divmod(h, PACK)
+            rows = slice(ROWS * g, ROWS * (g + 1))
+            bank = score_banks[g][bank_of(n)[1]]
+            tokens = slice(P * r, P * (r + 1))
+            for c in range(PACK):
+                cols = slice(P * c, P * (c + 1))
+                nc.tensor.matmul_mx(
+                    out=bank[:, cols],
+                    lhsT=codes["k", s][rows, tokens].bitcast(FP8X4),
+                    lhsT_scale=scales["k", s][rows, tokens],
+                    rhs=codes["q", s][rows, cols].bitcast(FP8X4),
+                    rhs_scale=scales["q", s][rows, cols],
+                    start=True,
+                    stop=True,
+                )
+
+        capped = {}
+        weights = {}
+        w_packed = {}
+        w_codes = {}
+        w_scales = {}
+
+        def cap(n):
+            h, r = order[n]
+            g, b = bank_of(n)
+            capped[n] = ring.tile([P, NQ], F32, name="capped", bufs=CAP_BUFS)
+            nc.scalar.activation(
+                out=capped[n][:], in_=score_banks[g][b][:], func=ACT.Tanh, bias=half_kb[:, r : r + 1], scale=0.5
+            )
+
+        def weigh(n):
+            h, r = order[n]
+            if r == 0:
+                weights[h] = ring.tile([P, PACK, NQ], BF16, name="weights", bufs=5)
+            nc.vector.tensor_scalar(
+                out=weights[h][:, r, :],
+                in0=capped[n][:],
+                scalar1=0.0,
+                scalar2=t_sb[:, r : r + 1],
+                op0=ALU.max,
+                op1=ALU.mult,
+            )
+
+        def pack_w(h, engine, lo, hi):
+            if h not in w_packed:
+                w_packed[h] = ring.tile([P, NQ, PACK], BF16, name="w_packed", bufs=3, align_bytes=64)
+            dst = w_packed[h][:].rearrange("p (a i) r -> p a r i", i=PACK)
+            src = weights[h][:].rearrange("p r (a i) -> p a r i", i=PACK)
+            copy_on(engine, dst[:, lo:hi], src[:, lo:hi])
+
+        def quantize_w(h, lo, hi):
+            if h not in w_codes:
+                w_codes[h] = ring.tile([P, NQ], U32, name="w_codes", bufs=4, align_bytes=64)
+                w_scales[h] = ring.tile([P, NQ], U8, name="w_scales", bufs=4, align_bytes=64)
+            nc.vector.quantize_mx(
+                out=w_codes[h][:, lo:hi].bitcast(FP8X4),
+                scales=w_scales[h][:, lo:hi],
+                in_=w_packed[h][:, lo:hi, :].rearrange("p n r -> p (n r)"),
+            )
+
+        def product(h, bank, lo, hi):
+            s, g = divmod(h, PACK)
+            feats = slice(P * g, P * (g + 1))
+            for c in range(lo, hi):
+                cols = slice(P * c, P * (c + 1))
+                nc.tensor.matmul_mx(
+                    out=out_banks[bank][:, cols],
+                    lhsT=w_codes[h][:, cols].bitcast(FP8X4),
+                    lhsT_scale=w_scales[h][:, cols],
+                    rhs=codes["v", s][:, feats].bitcast(FP8X4),
+                    rhs_scale=scales["v", s][:, feats],
+                    start=True,
+                    stop=True,
+                )
+
+        def store(h, bank, lo, hi):
+            cols = slice(P * lo, P * hi)
+            result = ring.tile([P, NQ], F32, name="result", bufs=3)
+            nc.scalar.activation(out=result[:, cols], in_=out_banks[bank][:, cols], func=ACT.Copy, scale=0.125)
+            nc.sync.dma_start(out=out[h].rearrange("(m c) e -> m (c e)", c=PACK)[:, cols], in_=result[:, cols])
+
+        nc.scalar.dma_start(out=kb_sb[:], in_=kb.rearrange("(p r) o -> p (r o)", r=PACK))
+        nc.scalar.dma_start(out=t_sb[:], in_=t.rearrange("(p r) o -> p (r o)", r=PACK))
+        for name, s in (("q", 0), ("k", 0), ("k", 1), ("q", 1), ("v", 0), ("v", 1)):
+            load(name, s)
+        nc.scalar.activation(out=warm[:], in_=kb_sb[:], func=ACT.Tanh)
+        nc.vector.tensor_scalar(out=half_kb[:], in0=kb_sb[:], scalar1=0.5, scalar2=None, op0=ALU.mult)
+        for name in ("q", "k"):
+            pack_dealt(name, 0, "vector", 0, HEAD_SPLIT)
+            pack_dealt(name, 0, "scalar", HEAD_SPLIT, 64)
+            if name == "q":
+                quantize(name, 0)
+        quantize("k", 0, 0, P)
+        quantize("k", 0, P, 2 * P)
+        quantize("k", 0, 2 * P, 4 * P)
+
+        last = H - 1
+        issued = 0
+        for n in range(-1, steps + PRODUCT_LAG + STORE_LAG):
+            if 0 <= n < steps:
+                cap(n)
+            h = done_at.get(n - PRODUCT_LAG)
+            if h is not None and h != last:
+                product(h, h % 2, 0, PACK)
+            while issued < min(steps, n + 4) and all(bank_of(m) != bank_of(issued) for m in range(n + 1, issued)):
+                scores(issued)
+                issued = issued + 1
+            h = done_at.get(n - PRODUCT_LAG - STORE_LAG)
+            if h is not None and h != last:
+                store(h, h % 2, 0, PACK)
+            if 0 <= n < steps:
+                weigh(n)
+            h = done_at.get(n - 1)
+            if h is not None:
+                split = SHARE if h >= SHARED_FROM else P
+                pack_w(h, "vector", 0, split)
+                if split < P:
+                    pack_w(h, "scalar", split, P)
+            h = done_at.get(n - 2)
+            if h is not None and h != last:
+                quantize_w(h, 0, NQ)
+            h = done_at.get(n + V_LEAD)
+            if h is not None:
+                pack_v(h // PACK, h % PACK, "scalar" if h < V_ON_SCALAR else "vector")
+            h = done_at.get(n + V_LEAD - V_GAP)
+            if h is not None:
+                quantize("v", h // PACK, P * (h % PACK), P * (h % PACK + 1))
+            if n == K1_STEP:
+                pack_dealt("k", 1, "vector", 0, 64)
+            if n == K1_STEP + 1:
+                quantize("k", 1)
+            if n == Q1_STEP:
+                pack_dealt("q", 1, "vector", 0, Q1_SPLIT)
+                if Q1_SPLIT < 64:
+                    pack_dealt("q", 1, "scalar", Q1_SPLIT, 64)
+            if n == Q1_STEP + 1:
+                quantize("q", 1)
+        for half in range(2):
+            quantize_w(last, 2 * P * half, 2 * P * (half + 1))
+            product(last, (last + half) % 2, 2 * half, 2 * half + 2)
+        for half in range(2):
+            store(last, (last + half) % 2, 2 * half, 2 * half + 2)

@@ -20,16 +20,26 @@ SETS = 2
 SKEW = 3
 HEAD_SPLIT = 40
 BANKS = (2, 1, 1, 2)
-PRODUCT_LAG = 5
-STORE_LAG = 1
-K1_STEP = 0
-Q1_STEP = 4
-V_LEAD = 0
-Q1_SPLIT = 48
-V_GAP = 2
-V_ON_SCALAR = 8
+PRODUCT_LAG = 6
+STORE_LAG = 3
+K1_STEP = 4
+Q1_STEP = 8
+V_LEAD = -1
+Q1_SPLIT = 12
+V_GAP = 1
+VS_LO = 1
+VS_HI = 8
+EARLY = 4
+HALVES = 1
+LOAD_ORDER = 0
+LOADS = [(("k", 0), ("q", 0), ("k", 1), ("q", 1), ("v", 0), ("v", 1)), (("k", 0), ("q", 0), ("k", 1), ("v", 0), ("q", 1), ("v", 1)), (("k", 0), ("q", 0), ("v", 0), ("k", 1), ("q", 1), ("v", 1))]
+Q0_SPLIT = 16
+Q0B_STEP = 0
+K1_SPLIT = 64
+SHARE_LAG = 3
+LAST_ENGINE = "vector"
 SHARED_FROM = 7
-SHARE = 64
+SHARE = 80
 CAP_BUFS = 12
 
 
@@ -47,14 +57,17 @@ def tile_rows_a_relu_kb_cap_kernel(tc, qT, kT, t, v, kb, out):
         kb_sb = kept("kb_sb", [P, PACK], F32)
         t_sb = kept("t_sb", [P, PACK], F32)
         half_kb = kept("half_kb", [P, PACK], F32)
-        warm = kept("warm", [P, PACK], F32)
         raw = {}
         packed = {}
         codes = {}
         scales = {}
         for name in ("k", "q", "v"):
             for s in range(SETS):
-                raw[name, s] = kept("raw_%s%d" % (name, s), [P, PACK, 512], F32)
+                if (name, s) != ("q", 0) or not HALVES:
+                    raw[name, s] = kept("raw_%s%d" % (name, s), [P, PACK, 512], F32)
+                else:
+                    for half in range(2):
+                        raw[name, s, half] = kept("raw_%s%d%d" % (name, s, half), [P, PACK, 256], F32)
                 packed[name, s] = kept("packed_%s%d" % (name, s), [P, 512, PACK], BF16)
                 codes[name, s] = kept("codes_%s%d" % (name, s), [P, 512], U32)
                 scales[name, s] = kept("scales_%s%d" % (name, s), [P, 512], U8)
@@ -66,10 +79,14 @@ def tile_rows_a_relu_kb_cap_kernel(tc, qT, kT, t, v, kb, out):
         def load(name, s):
             heads = slice(PACK * s, PACK * (s + 1))
             if name == "v":
-                src = v[heads].rearrange("h (p r) e -> p h (r e)", r=PACK)
-            else:
+                nc.sync.dma_start(out=raw[name, s][:], in_=v[heads].rearrange("h (p r) e -> p h (r e)", r=PACK))
+            elif (name, s) != ("q", 0) or not HALVES:
                 src = (kT if name == "k" else qT)[heads].rearrange("h (p j) n -> (h p) j n", j=PACK)
-            nc.sync.dma_start(out=raw[name, s][:], in_=src)
+                nc.sync.dma_start(out=raw[name, s][:], in_=src)
+            else:
+                src = qT[heads].rearrange("h (p j) n -> (h p) j n", j=PACK)
+                for half in range(2):
+                    nc.sync.dma_start(out=raw[name, s, half][:], in_=src[:, :, 256 * half : 256 * (half + 1)])
 
         def copy_on(engine, dst, src):
             if engine == "vector":
@@ -80,6 +97,12 @@ def tile_rows_a_relu_kb_cap_kernel(tc, qT, kT, t, v, kb, out):
         def pack_dealt(name, s, engine, lo, hi):
             dst = packed[name, s][:].rearrange("p (c a b) j -> p a j b c", c=PACK, b=2)
             src = raw[name, s][:].rearrange("p j (a b c) -> p a j b c", c=PACK, b=2)
+            copy_on(engine, dst[:, lo:hi], src[:, lo:hi])
+
+        def pack_q(s, half, engine, lo, hi):
+            dst = packed["q", s][:, 256 * half : 256 * (half + 1), :].rearrange("p (c a b) j -> p a j b c", c=PACK, b=2)
+            rows = raw["q", s, half][:] if s == 0 and HALVES else raw["q", s][:, :, 256 * half : 256 * (half + 1)]
+            src = rows.rearrange("p j (a b c) -> p a j b c", c=PACK, b=2)
             copy_on(engine, dst[:, lo:hi], src[:, lo:hi])
 
         def pack_v(s, g, engine):
@@ -94,22 +117,25 @@ def tile_rows_a_relu_kb_cap_kernel(tc, qT, kT, t, v, kb, out):
                 in_=packed[name, s][:, lo:hi, :].rearrange("p n j -> p (n j)"),
             )
 
-        order = [(h, r) for key, h, r in sorted((PACK * h + SKEW * r, h, r) for h in range(H) for r in range(PACK))]
+        tiles = [(h, r) for key, h, r in sorted((PACK * h + SKEW * r, h, r) for h in range(H) for r in range(PACK))]
+        early = [(0, 0), (0, 1), (1, 0), (2, 0), (3, 0)][:EARLY]
+        order = [(h, r, half, half + 1) for half in range(2) for h, r in early]
+        order = order + [(h, r, 0, 2) for h, r in tiles if (h, r) not in early]
         steps = len(order)
-        done_at = {order.index((h, PACK - 1)): h for h in range(H)}
+        done_at = {order.index((h, PACK - 1, 0, 2)): h for h in range(H)}
 
         def bank_of(n):
-            h, r = order[n]
+            h, r, lo, hi = order[n]
             g = h % PACK
             return g, r % BANKS[g]
 
         def scores(n):
-            h, r = order[n]
+            h, r, lo, hi = order[n]
             s, g = divmod(h, PACK)
             rows = slice(ROWS * g, ROWS * (g + 1))
             bank = score_banks[g][bank_of(n)[1]]
             tokens = slice(P * r, P * (r + 1))
-            for c in range(PACK):
+            for c in range(2 * lo, 2 * hi):
                 cols = slice(P * c, P * (c + 1))
                 nc.tensor.matmul_mx(
                     out=bank[:, cols],
@@ -128,20 +154,21 @@ def tile_rows_a_relu_kb_cap_kernel(tc, qT, kT, t, v, kb, out):
         w_scales = {}
 
         def cap(n):
-            h, r = order[n]
+            h, r, lo, hi = order[n]
             g, b = bank_of(n)
             capped[n] = ring.tile([P, NQ], F32, name="capped", bufs=CAP_BUFS)
+            cols = slice(256 * lo, 256 * hi)
             nc.scalar.activation(
-                out=capped[n][:], in_=score_banks[g][b][:], func=ACT.Tanh, bias=half_kb[:, r : r + 1], scale=0.5
+                out=capped[n][:, cols], in_=score_banks[g][b][:, cols], func=ACT.Tanh, bias=half_kb[:, r : r + 1], scale=0.5
             )
 
         def weigh(n):
-            h, r = order[n]
-            if r == 0:
-                weights[h] = ring.tile([P, PACK, NQ], BF16, name="weights", bufs=5)
+            h, r, lo, hi = order[n]
+            if h not in weights:
+                weights[h] = ring.tile([P, PACK, NQ], BF16, name="weights", bufs=6)
             nc.vector.tensor_scalar(
-                out=weights[h][:, r, :],
-                in0=capped[n][:],
+                out=weights[h][:, r, :].rearrange("p (c u m) -> p u c m", c=PACK, u=2)[:, lo:hi],
+                in0=capped[n][:].rearrange("p (u c m) -> p u c m", c=PACK, u=2)[:, lo:hi],
                 scalar1=0.0,
                 scalar2=t_sb[:, r : r + 1],
                 op0=ALU.max,
@@ -180,36 +207,44 @@ def tile_rows_a_relu_kb_cap_kernel(tc, qT, kT, t, v, kb, out):
                     stop=True,
                 )
 
-        def store(h, bank, lo, hi):
+        def store(h, bank, lo, hi, engine="scalar"):
             cols = slice(P * lo, P * hi)
-            result = ring.tile([P, NQ], F32, name="result", bufs=3)
-            nc.scalar.activation(out=result[:, cols], in_=out_banks[bank][:, cols], func=ACT.Copy, scale=0.125)
+            result = ring.tile([P, NQ], F32, name="result", bufs=4)
+            if engine == "scalar":
+                nc.scalar.activation(out=result[:, cols], in_=out_banks[bank][:, cols], func=ACT.Copy, scale=0.125)
+            else:
+                nc.vector.tensor_scalar(out=result[:, cols], in0=out_banks[bank][:, cols], scalar1=0.125, scalar2=None, op0=ALU.mult)
             nc.sync.dma_start(out=out[h].rearrange("(m c) e -> m (c e)", c=PACK)[:, cols], in_=result[:, cols])
 
         nc.scalar.dma_start(out=kb_sb[:], in_=kb.rearrange("(p r) o -> p (r o)", r=PACK))
         nc.scalar.dma_start(out=t_sb[:], in_=t.rearrange("(p r) o -> p (r o)", r=PACK))
-        for name, s in (("q", 0), ("k", 0), ("k", 1), ("q", 1), ("v", 0), ("v", 1)):
+        for name, s in LOADS[LOAD_ORDER]:
             load(name, s)
-        nc.scalar.activation(out=warm[:], in_=kb_sb[:], func=ACT.Tanh)
-        nc.vector.tensor_scalar(out=half_kb[:], in0=kb_sb[:], scalar1=0.5, scalar2=None, op0=ALU.mult)
-        for name in ("q", "k"):
-            pack_dealt(name, 0, "vector", 0, HEAD_SPLIT)
-            pack_dealt(name, 0, "scalar", HEAD_SPLIT, 64)
-            if name == "q":
-                quantize(name, 0)
-        quantize("k", 0, 0, P)
-        quantize("k", 0, P, 2 * P)
-        quantize("k", 0, 2 * P, 4 * P)
+        nc.scalar.activation(out=half_kb[:], in_=kb_sb[:], func=ACT.Copy, scale=0.5)
+        pack_dealt("k", 0, "vector", 0, HEAD_SPLIT)
+        pack_dealt("k", 0, "scalar", HEAD_SPLIT, 64)
+        quantize("k", 0)
+        pack_q(0, 0, "vector", 0, Q0_SPLIT)
+        pack_q(0, 0, "scalar", Q0_SPLIT, 32)
+        quantize("q", 0, 0, 256)
+        pack_q(0, 1, "vector", 0, 32)
 
         last = H - 1
         issued = 0
+        base = 2 * EARLY
         for n in range(-1, steps + PRODUCT_LAG + STORE_LAG):
             if 0 <= n < steps:
                 cap(n)
+            if n == Q0B_STEP:
+                quantize("q", 0, 256, 512)
             h = done_at.get(n - PRODUCT_LAG)
             if h is not None and h != last:
                 product(h, h % 2, 0, PACK)
-            while issued < min(steps, n + 4) and all(bank_of(m) != bank_of(issued) for m in range(n + 1, issued)):
+            while (
+                issued < min(steps, n + 4)
+                and all(bank_of(m) != bank_of(issued) for m in range(n + 1, issued))
+                and (issued < EARLY or n >= Q0B_STEP)
+            ):
                 scores(issued)
                 issued = issued + 1
             h = done_at.get(n - PRODUCT_LAG - STORE_LAG)
@@ -219,31 +254,38 @@ def tile_rows_a_relu_kb_cap_kernel(tc, qT, kT, t, v, kb, out):
                 weigh(n)
             h = done_at.get(n - 1)
             if h is not None:
-                split = SHARE if h >= SHARED_FROM else P
-                pack_w(h, "vector", 0, split)
-                if split < P:
-                    pack_w(h, "scalar", split, P)
+                pack_w(h, "vector", 0, SHARE if h >= SHARED_FROM else P)
+            h = done_at.get(n - SHARE_LAG)
+            if h is not None and h >= SHARED_FROM and SHARE < P:
+                pack_w(h, "scalar", SHARE, P)
             h = done_at.get(n - 2)
-            if h is not None and h != last:
+            if h is not None and h < SHARED_FROM:
+                quantize_w(h, 0, NQ)
+            h = done_at.get(n - max(2, SHARE_LAG))
+            if h is not None and SHARED_FROM <= h < last:
                 quantize_w(h, 0, NQ)
             h = done_at.get(n + V_LEAD)
             if h is not None:
-                pack_v(h // PACK, h % PACK, "scalar" if h < V_ON_SCALAR else "vector")
+                pack_v(h // PACK, h % PACK, "scalar" if VS_LO <= h < VS_HI else "vector")
             h = done_at.get(n + V_LEAD - V_GAP)
             if h is not None:
                 quantize("v", h // PACK, P * (h % PACK), P * (h % PACK + 1))
             if n == K1_STEP:
-                pack_dealt("k", 1, "vector", 0, 64)
+                pack_dealt("k", 1, "vector", 0, K1_SPLIT)
+                if K1_SPLIT < 64:
+                    pack_dealt("k", 1, "scalar", K1_SPLIT, 64)
             if n == K1_STEP + 1:
                 quantize("k", 1)
             if n == Q1_STEP:
-                pack_dealt("q", 1, "vector", 0, Q1_SPLIT)
-                if Q1_SPLIT < 64:
-                    pack_dealt("q", 1, "scalar", Q1_SPLIT, 64)
+                pack_q(1, 0, "vector", 0, 32)
             if n == Q1_STEP + 1:
+                pack_q(1, 1, "vector", 0, Q1_SPLIT)
+                if Q1_SPLIT < 32:
+                    pack_q(1, 1, "scalar", Q1_SPLIT, 32)
+            if n == Q1_STEP + 2:
                 quantize("q", 1)
         for half in range(2):
             quantize_w(last, 2 * P * half, 2 * P * (half + 1))
             product(last, (last + half) % 2, 2 * half, 2 * half + 2)
-        for half in range(2):
-            store(last, (last + half) % 2, 2 * half, 2 * half + 2)
+        store(last, last % 2, 0, 2)
+        store(last, (last + 1) % 2, 2, 4, LAST_ENGINE)

@@ -18,28 +18,29 @@ PACK = 4
 ROWS = 32
 SETS = 2
 SKEW = 3
-HEAD_SPLIT = 40
+HEAD_SPLIT = 0
 BANKS = (2, 1, 1, 2)
-PRODUCT_LAG = 6
+PRODUCT_LAG = 7
 STORE_LAG = 3
 K1_STEP = 4
-Q1_STEP = 8
+Q1_STEP = 9
 V_LEAD = -1
-Q1_SPLIT = 12
+Q1_SPLIT = 32
 V_GAP = 1
 VS_LO = 1
 VS_HI = 8
 EARLY = 4
+Q1A_SPLIT = 32
 HALVES = 1
 LOAD_ORDER = 0
 LOADS = [(("k", 0), ("q", 0), ("k", 1), ("q", 1), ("v", 0), ("v", 1)), (("k", 0), ("q", 0), ("k", 1), ("v", 0), ("q", 1), ("v", 1)), (("k", 0), ("q", 0), ("v", 0), ("k", 1), ("q", 1), ("v", 1))]
-Q0_SPLIT = 16
+Q0_SPLIT = 0
 Q0B_STEP = 0
 K1_SPLIT = 64
 SHARE_LAG = 3
 LAST_ENGINE = "vector"
 SHARED_FROM = 7
-SHARE = 80
+SHARE = 128
 CAP_BUFS = 12
 
 
@@ -94,16 +95,20 @@ def tile_rows_a_relu_kb_cap_kernel(tc, qT, kT, t, v, kb, out):
             else:
                 nc.scalar.copy(out=dst, in_=src)
 
-        def pack_dealt(name, s, engine, lo, hi):
-            dst = packed[name, s][:].rearrange("p (c a b) j -> p a j b c", c=PACK, b=2)
-            src = raw[name, s][:].rearrange("p j (a b c) -> p a j b c", c=PACK, b=2)
-            copy_on(engine, dst[:, lo:hi], src[:, lo:hi])
+        def pack_pairs(dst, src, pair, split):
+            dst = dst.rearrange("p (c a b) j -> p a j b c", c=PACK, b=2)[:, :, :, :, 2 * pair : 2 * pair + 2]
+            src = src.rearrange("p j (a b c) -> p a j b c", c=PACK, b=2)[:, :, :, :, 2 * pair : 2 * pair + 2]
+            if split > 0:
+                copy_on("vector", dst[:, :split], src[:, :split])
+            if split < dst.shape[1]:
+                copy_on("scalar", dst[:, split:], src[:, split:])
 
-        def pack_q(s, half, engine, lo, hi):
-            dst = packed["q", s][:, 256 * half : 256 * (half + 1), :].rearrange("p (c a b) j -> p a j b c", c=PACK, b=2)
+        def pack_k(s, pair, split):
+            pack_pairs(packed["k", s][:], raw["k", s][:], pair, split)
+
+        def pack_q(s, half, pair, split):
             rows = raw["q", s, half][:] if s == 0 and HALVES else raw["q", s][:, :, 256 * half : 256 * (half + 1)]
-            src = rows.rearrange("p j (a b c) -> p a j b c", c=PACK, b=2)
-            copy_on(engine, dst[:, lo:hi], src[:, lo:hi])
+            pack_pairs(packed["q", s][:, 256 * half : 256 * (half + 1), :], rows, pair, split)
 
         def pack_v(s, g, engine):
             dst = packed["v", s][:, P * g : P * (g + 1), :].rearrange("p (a i) r -> p a r i", i=PACK)
@@ -165,9 +170,9 @@ def tile_rows_a_relu_kb_cap_kernel(tc, qT, kT, t, v, kb, out):
         def weigh(n):
             h, r, lo, hi = order[n]
             if h not in weights:
-                weights[h] = ring.tile([P, PACK, NQ], BF16, name="weights", bufs=6)
+                weights[h] = ring.tile([P, 2, NQ, 2], BF16, name="weights", bufs=6)
             nc.vector.tensor_scalar(
-                out=weights[h][:, r, :].rearrange("p (c u m) -> p u c m", c=PACK, u=2)[:, lo:hi],
+                out=weights[h][:, r // 2, :, r % 2].rearrange("p (c u m) -> p u c m", c=PACK, u=2)[:, lo:hi],
                 in0=capped[n][:].rearrange("p (u c m) -> p u c m", c=PACK, u=2)[:, lo:hi],
                 scalar1=0.0,
                 scalar2=t_sb[:, r : r + 1],
@@ -178,9 +183,9 @@ def tile_rows_a_relu_kb_cap_kernel(tc, qT, kT, t, v, kb, out):
         def pack_w(h, engine, lo, hi):
             if h not in w_packed:
                 w_packed[h] = ring.tile([P, NQ, PACK], BF16, name="w_packed", bufs=3, align_bytes=64)
-            dst = w_packed[h][:].rearrange("p (a i) r -> p a r i", i=PACK)
-            src = weights[h][:].rearrange("p r (a i) -> p a r i", i=PACK)
-            copy_on(engine, dst[:, lo:hi], src[:, lo:hi])
+            dst = w_packed[h][:].rearrange("p n r -> p (n r)").bitcast(F32).rearrange("p (a i u) -> p a u i", i=2, u=2)
+            src = weights[h][:].rearrange("p u n e -> p (u n e)").bitcast(F32).rearrange("p (u a i) -> p a u i", i=2, u=2)
+            copy_on(engine, dst[:, 2 * lo : 2 * hi], src[:, 2 * lo : 2 * hi])
 
         def quantize_w(h, lo, hi):
             if h not in w_codes:
@@ -221,13 +226,15 @@ def tile_rows_a_relu_kb_cap_kernel(tc, qT, kT, t, v, kb, out):
         for name, s in LOADS[LOAD_ORDER]:
             load(name, s)
         nc.scalar.activation(out=half_kb[:], in_=kb_sb[:], func=ACT.Copy, scale=0.5)
-        pack_dealt("k", 0, "vector", 0, HEAD_SPLIT)
-        pack_dealt("k", 0, "scalar", HEAD_SPLIT, 64)
-        quantize("k", 0)
-        pack_q(0, 0, "vector", 0, Q0_SPLIT)
-        pack_q(0, 0, "scalar", Q0_SPLIT, 32)
+        pack_k(0, 0, 64)
+        pack_k(0, 1, HEAD_SPLIT)
+        quantize("k", 0, 0, 256)
+        pack_q(0, 0, 0, 32)
+        pack_q(0, 0, 1, Q0_SPLIT)
+        quantize("k", 0, 256, 512)
         quantize("q", 0, 0, 256)
-        pack_q(0, 1, "vector", 0, 32)
+        pack_q(0, 1, 0, 32)
+        pack_q(0, 1, 1, 32)
 
         last = H - 1
         issued = 0
@@ -254,7 +261,8 @@ def tile_rows_a_relu_kb_cap_kernel(tc, qT, kT, t, v, kb, out):
                 weigh(n)
             h = done_at.get(n - 1)
             if h is not None:
-                pack_w(h, "vector", 0, SHARE if h >= SHARED_FROM else P)
+                if SHARE or h < SHARED_FROM:
+                    pack_w(h, "vector", 0, SHARE if h >= SHARED_FROM else P)
             h = done_at.get(n - SHARE_LAG)
             if h is not None and h >= SHARED_FROM and SHARE < P:
                 pack_w(h, "scalar", SHARE, P)
@@ -271,17 +279,16 @@ def tile_rows_a_relu_kb_cap_kernel(tc, qT, kT, t, v, kb, out):
             if h is not None:
                 quantize("v", h // PACK, P * (h % PACK), P * (h % PACK + 1))
             if n == K1_STEP:
-                pack_dealt("k", 1, "vector", 0, K1_SPLIT)
-                if K1_SPLIT < 64:
-                    pack_dealt("k", 1, "scalar", K1_SPLIT, 64)
+                pack_k(1, 0, 64)
+                pack_k(1, 1, K1_SPLIT)
             if n == K1_STEP + 1:
                 quantize("k", 1)
             if n == Q1_STEP:
-                pack_q(1, 0, "vector", 0, 32)
+                pack_q(1, 0, 0, 32)
+                pack_q(1, 0, 1, Q1A_SPLIT)
             if n == Q1_STEP + 1:
-                pack_q(1, 1, "vector", 0, Q1_SPLIT)
-                if Q1_SPLIT < 32:
-                    pack_q(1, 1, "scalar", Q1_SPLIT, 32)
+                pack_q(1, 1, 0, Q1_SPLIT)
+                pack_q(1, 1, 1, 0)
             if n == Q1_STEP + 2:
                 quantize("q", 1)
         for half in range(2):

@@ -16,32 +16,20 @@ ALU = mybir.AluOpType
 P = 128
 PACK = 4
 ROWS = 32
-SETS = 2
+SETS = H // PACK
+COLS = 512
+HALF = NQ // 2
+OUT_SCALE = 2.0 / 16.0
+
 SKEW = 3
-HEAD_SPLIT = 0
-BANKS = (2, 1, 1, 2)
-PRODUCT_LAG = 7
+SCORE_BANKS = (2, 1, 1, 2)
+OUT_BANKS = 2
+AHEAD = 3
+EARLY_TILES = ((0, 0), (0, 1), (1, 0), (2, 0))
+PRODUCT_LAG = 8
 STORE_LAG = 3
-K1_STEP = 4
-Q1_STEP = 9
-V_LEAD = -1
-Q1_SPLIT = 32
-V_GAP = 1
-VS_LO = 1
-VS_HI = 8
-EARLY = 4
-Q1A_SPLIT = 32
-HALVES = 1
-LOAD_ORDER = 0
-LOADS = [(("k", 0), ("q", 0), ("k", 1), ("q", 1), ("v", 0), ("v", 1)), (("k", 0), ("q", 0), ("k", 1), ("v", 0), ("q", 1), ("v", 1)), (("k", 0), ("q", 0), ("v", 0), ("k", 1), ("q", 1), ("v", 1))]
-Q0_SPLIT = 0
-Q0B_STEP = 0
-K1_SPLIT = 64
-SHARE_LAG = 3
-LAST_ENGINE = "vector"
-SHARED_FROM = 7
-SHARE = 128
-CAP_BUFS = 12
+K_STEP = 4
+Q_STEP = 9
 
 
 def tile_rows_a_relu_kb_cap_kernel(tc, qT, kT, t, v, kb, out):
@@ -58,36 +46,29 @@ def tile_rows_a_relu_kb_cap_kernel(tc, qT, kT, t, v, kb, out):
         kb_sb = kept("kb_sb", [P, PACK], F32)
         t_sb = kept("t_sb", [P, PACK], F32)
         half_kb = kept("half_kb", [P, PACK], F32)
-        raw = {}
-        packed = {}
-        codes = {}
-        scales = {}
+        raw, packed, codes, scales = {}, {}, {}, {}
         for name in ("k", "q", "v"):
             for s in range(SETS):
-                if (name, s) != ("q", 0) or not HALVES:
-                    raw[name, s] = kept("raw_%s%d" % (name, s), [P, PACK, 512], F32)
+                if (name, s) == ("q", 0):
+                    first_q = [kept("raw_q0%d" % u, [P, PACK, HALF], F32) for u in range(2)]
                 else:
-                    for half in range(2):
-                        raw[name, s, half] = kept("raw_%s%d%d" % (name, s, half), [P, PACK, 256], F32)
-                packed[name, s] = kept("packed_%s%d" % (name, s), [P, 512, PACK], BF16)
-                codes[name, s] = kept("codes_%s%d" % (name, s), [P, 512], U32)
-                scales[name, s] = kept("scales_%s%d" % (name, s), [P, 512], U8)
+                    raw[name, s] = kept("raw_%s%d" % (name, s), [P, PACK, COLS], F32)
+                packed[name, s] = kept("packed_%s%d" % (name, s), [P, COLS, PACK], BF16)
+                codes[name, s] = kept("codes_%s%d" % (name, s), [P, COLS], U32)
+                scales[name, s] = kept("scales_%s%d" % (name, s), [P, COLS], U8)
         score_banks = [
-            [psum.tile([P, NQ], F32, name="score_%d_%d" % (g, b)) for b in range(BANKS[g])] for g in range(PACK)
+            [psum.tile([P, NQ], F32, name="score_%d_%d" % (g, b)) for b in range(SCORE_BANKS[g])] for g in range(PACK)
         ]
-        out_banks = [psum.tile([P, NQ], F32, name="out_bank_%d" % b) for b in range(2)]
+        out_banks = [psum.tile([P, NQ], F32, name="out_bank_%d" % b) for b in range(OUT_BANKS)]
 
-        def load(name, s):
-            heads = slice(PACK * s, PACK * (s + 1))
-            if name == "v":
-                nc.sync.dma_start(out=raw[name, s][:], in_=v[heads].rearrange("h (p r) e -> p h (r e)", r=PACK))
-            elif (name, s) != ("q", 0) or not HALVES:
-                src = (kT if name == "k" else qT)[heads].rearrange("h (p j) n -> (h p) j n", j=PACK)
-                nc.sync.dma_start(out=raw[name, s][:], in_=src)
-            else:
-                src = qT[heads].rearrange("h (p j) n -> (h p) j n", j=PACK)
-                for half in range(2):
-                    nc.sync.dma_start(out=raw[name, s, half][:], in_=src[:, :, 256 * half : 256 * (half + 1)])
+        def features_view(x, s):
+            return x[PACK * s : PACK * (s + 1)].rearrange("h (p j) n -> (h p) j n", j=PACK)
+
+        def tokens_view(s):
+            return v[PACK * s : PACK * (s + 1)].rearrange("h (p r) e -> p h (r e)", r=PACK)
+
+        def half_cols(u):
+            return slice(HALF * u, HALF * (u + 1))
 
         def copy_on(engine, dst, src):
             if engine == "vector":
@@ -95,55 +76,53 @@ def tile_rows_a_relu_kb_cap_kernel(tc, qT, kT, t, v, kb, out):
             else:
                 nc.scalar.copy(out=dst, in_=src)
 
-        def pack_pairs(dst, src, pair, split):
-            dst = dst.rearrange("p (c a b) j -> p a j b c", c=PACK, b=2)[:, :, :, :, 2 * pair : 2 * pair + 2]
-            src = src.rearrange("p j (a b c) -> p a j b c", c=PACK, b=2)[:, :, :, :, 2 * pair : 2 * pair + 2]
-            if split > 0:
-                copy_on("vector", dst[:, :split], src[:, :split])
-            if split < dst.shape[1]:
-                copy_on("scalar", dst[:, split:], src[:, split:])
+        def pack_dealt(dst, src, pair, engines):
+            places = slice(2 * pair, 2 * pair + 2)
+            dst = dst.rearrange("p (c a b) j -> p a j b c", c=PACK, b=2)[:, :, :, :, places]
+            src = src.rearrange("p j (a b c) -> p a j b c", c=PACK, b=2)[:, :, :, :, places]
+            share = dst.shape[1] // len(engines)
+            for i, engine in enumerate(engines):
+                copy_on(engine, dst[:, share * i : share * (i + 1)], src[:, share * i : share * (i + 1)])
 
-        def pack_k(s, pair, split):
-            pack_pairs(packed["k", s][:], raw["k", s][:], pair, split)
+        def pack_k(s, pair, *engines):
+            pack_dealt(packed["k", s][:], raw["k", s][:], pair, engines)
 
-        def pack_q(s, half, pair, split):
-            rows = raw["q", s, half][:] if s == 0 and HALVES else raw["q", s][:, :, 256 * half : 256 * (half + 1)]
-            pack_pairs(packed["q", s][:, 256 * half : 256 * (half + 1), :], rows, pair, split)
+        def pack_q(s, u, pair, *engines):
+            src = first_q[u][:] if s == 0 else raw["q", s][:, :, half_cols(u)]
+            pack_dealt(packed["q", s][:, half_cols(u), :], src, pair, engines)
 
-        def pack_v(s, g, engine):
+        def pack_v(h, engine):
+            s, g = divmod(h, PACK)
             dst = packed["v", s][:, P * g : P * (g + 1), :].rearrange("p (a i) r -> p a r i", i=PACK)
             src = raw["v", s][:, g, :].rearrange("p (r a i) -> p a r i", r=PACK, i=PACK)
             copy_on(engine, dst, src)
 
-        def quantize(name, s, lo=0, hi=512):
+        def quantize(name, s, lo=0, hi=COLS):
             nc.vector.quantize_mx(
                 out=codes[name, s][:, lo:hi].bitcast(FP8X4),
                 scales=scales[name, s][:, lo:hi],
                 in_=packed[name, s][:, lo:hi, :].rearrange("p n j -> p (n j)"),
             )
 
-        tiles = [(h, r) for key, h, r in sorted((PACK * h + SKEW * r, h, r) for h in range(H) for r in range(PACK))]
-        early = [(0, 0), (0, 1), (1, 0), (2, 0), (3, 0)][:EARLY]
-        order = [(h, r, half, half + 1) for half in range(2) for h, r in early]
-        order = order + [(h, r, 0, 2) for h, r in tiles if (h, r) not in early]
+        tiles = sorted(((h, r) for h in range(H) for r in range(PACK)), key=lambda hr: PACK * hr[0] + SKEW * hr[1])
+        order = [(h, r, u, u + 1) for u in range(2) for h, r in EARLY_TILES]
+        order = order + [(h, r, 0, 2) for h, r in tiles if (h, r) not in EARLY_TILES]
         steps = len(order)
-        done_at = {order.index((h, PACK - 1, 0, 2)): h for h in range(H)}
+        ends_at = {order.index((h, PACK - 1, 0, 2)): h for h in range(H)}
 
         def bank_of(n):
             h, r, lo, hi = order[n]
-            g = h % PACK
-            return g, r % BANKS[g]
+            return h % PACK, r % SCORE_BANKS[h % PACK]
 
         def scores(n):
             h, r, lo, hi = order[n]
             s, g = divmod(h, PACK)
             rows = slice(ROWS * g, ROWS * (g + 1))
-            bank = score_banks[g][bank_of(n)[1]]
             tokens = slice(P * r, P * (r + 1))
-            for c in range(2 * lo, 2 * hi):
-                cols = slice(P * c, P * (c + 1))
+            for block in range(2 * lo, 2 * hi):
+                cols = slice(P * block, P * (block + 1))
                 nc.tensor.matmul_mx(
-                    out=bank[:, cols],
+                    out=score_banks[g][bank_of(n)[1]][:, cols],
                     lhsT=codes["k", s][rows, tokens].bitcast(FP8X4),
                     lhsT_scale=scales["k", s][rows, tokens],
                     rhs=codes["q", s][rows, cols].bitcast(FP8X4),
@@ -152,27 +131,27 @@ def tile_rows_a_relu_kb_cap_kernel(tc, qT, kT, t, v, kb, out):
                     stop=True,
                 )
 
-        capped = {}
-        weights = {}
-        w_packed = {}
-        w_codes = {}
-        w_scales = {}
+        capped, paired, w_packed, w_codes, w_scales = {}, {}, {}, {}, {}
 
         def cap(n):
             h, r, lo, hi = order[n]
             g, b = bank_of(n)
-            capped[n] = ring.tile([P, NQ], F32, name="capped", bufs=CAP_BUFS)
-            cols = slice(256 * lo, 256 * hi)
+            capped[n] = ring.tile([P, NQ], F32, name="capped", bufs=12)
+            cols = slice(HALF * lo, HALF * hi)
             nc.scalar.activation(
-                out=capped[n][:, cols], in_=score_banks[g][b][:, cols], func=ACT.Tanh, bias=half_kb[:, r : r + 1], scale=0.5
+                out=capped[n][:, cols],
+                in_=score_banks[g][b][:, cols],
+                func=ACT.Tanh,
+                bias=half_kb[:, r : r + 1],
+                scale=0.5,
             )
 
         def weigh(n):
             h, r, lo, hi = order[n]
-            if h not in weights:
-                weights[h] = ring.tile([P, 2, NQ, 2], BF16, name="weights", bufs=6)
+            if h not in paired:
+                paired[h] = ring.tile([P, 2, NQ, 2], BF16, name="paired", bufs=6)
             nc.vector.tensor_scalar(
-                out=weights[h][:, r // 2, :, r % 2].rearrange("p (c u m) -> p u c m", c=PACK, u=2)[:, lo:hi],
+                out=paired[h][:, r // 2, :, r % 2].rearrange("p (c u m) -> p u c m", c=PACK, u=2)[:, lo:hi],
                 in0=capped[n][:].rearrange("p (u c m) -> p u c m", c=PACK, u=2)[:, lo:hi],
                 scalar1=0.0,
                 scalar2=t_sb[:, r : r + 1],
@@ -180,21 +159,24 @@ def tile_rows_a_relu_kb_cap_kernel(tc, qT, kT, t, v, kb, out):
                 op1=ALU.mult,
             )
 
-        def pack_w(h, engine, lo, hi):
-            if h not in w_packed:
-                w_packed[h] = ring.tile([P, NQ, PACK], BF16, name="w_packed", bufs=3, align_bytes=64)
-            dst = w_packed[h][:].rearrange("p n r -> p (n r)").bitcast(F32).rearrange("p (a i u) -> p a u i", i=2, u=2)
-            src = weights[h][:].rearrange("p u n e -> p (u n e)").bitcast(F32).rearrange("p (u a i) -> p a u i", i=2, u=2)
-            copy_on(engine, dst[:, 2 * lo : 2 * hi], src[:, 2 * lo : 2 * hi])
+        def pack_w(h):
+            w_packed[h] = ring.tile([P, NQ, PACK], BF16, name="w_packed", bufs=3, align_bytes=64)
+            dst = w_packed[h][:].rearrange("p n r -> p (n r)").bitcast(F32)
+            src = paired[h][:].rearrange("p x n y -> p (x n y)").bitcast(F32)
+            nc.vector.tensor_copy(
+                out=dst.rearrange("p (a i x) -> p a x i", i=2, x=2),
+                in_=src.rearrange("p (x a i) -> p a x i", i=2, x=2),
+            )
 
         def quantize_w(h, lo, hi):
             if h not in w_codes:
-                w_codes[h] = ring.tile([P, NQ], U32, name="w_codes", bufs=4, align_bytes=64)
-                w_scales[h] = ring.tile([P, NQ], U8, name="w_scales", bufs=4, align_bytes=64)
+                w_codes[h] = ring.tile([P, NQ], U32, name="w_codes", align_bytes=64)
+                w_scales[h] = ring.tile([P, NQ], U8, name="w_scales", align_bytes=64)
+            cols = slice(P * lo, P * hi)
             nc.vector.quantize_mx(
-                out=w_codes[h][:, lo:hi].bitcast(FP8X4),
-                scales=w_scales[h][:, lo:hi],
-                in_=w_packed[h][:, lo:hi, :].rearrange("p n r -> p (n r)"),
+                out=w_codes[h][:, cols].bitcast(FP8X4),
+                scales=w_scales[h][:, cols],
+                in_=w_packed[h][:, cols, :].rearrange("p n r -> p (n r)"),
             )
 
         def product(h, bank, lo, hi):
@@ -212,87 +194,86 @@ def tile_rows_a_relu_kb_cap_kernel(tc, qT, kT, t, v, kb, out):
                     stop=True,
                 )
 
-        def store(h, bank, lo, hi, engine="scalar"):
+        def store(h, bank, lo, hi, engine):
             cols = slice(P * lo, P * hi)
-            result = ring.tile([P, NQ], F32, name="result", bufs=4)
+            result = ring.tile([P, NQ], F32, name="result", bufs=5)
             if engine == "scalar":
-                nc.scalar.activation(out=result[:, cols], in_=out_banks[bank][:, cols], func=ACT.Copy, scale=0.125)
+                nc.scalar.activation(out=result[:, cols], in_=out_banks[bank][:, cols], func=ACT.Copy, scale=OUT_SCALE)
             else:
-                nc.vector.tensor_scalar(out=result[:, cols], in0=out_banks[bank][:, cols], scalar1=0.125, scalar2=None, op0=ALU.mult)
-            nc.sync.dma_start(out=out[h].rearrange("(m c) e -> m (c e)", c=PACK)[:, cols], in_=result[:, cols])
+                nc.vector.tensor_scalar(
+                    out=result[:, cols], in0=out_banks[bank][:, cols], scalar1=OUT_SCALE, scalar2=None, op0=ALU.mult
+                )
+            nc.sync.dma_start(out=out[h].rearrange("(n c) e -> n (c e)", c=PACK)[:, cols], in_=result[:, cols])
 
         nc.scalar.dma_start(out=kb_sb[:], in_=kb.rearrange("(p r) o -> p (r o)", r=PACK))
         nc.scalar.dma_start(out=t_sb[:], in_=t.rearrange("(p r) o -> p (r o)", r=PACK))
-        for name, s in LOADS[LOAD_ORDER]:
-            load(name, s)
+        nc.sync.dma_start(out=first_q[0][:], in_=features_view(qT, 0)[:, :, half_cols(0)])
+        nc.sync.dma_start(out=raw["k", 0][:], in_=features_view(kT, 0))
+        nc.sync.dma_start(out=first_q[1][:], in_=features_view(qT, 0)[:, :, half_cols(1)])
+        nc.sync.dma_start(out=raw["k", 1][:], in_=features_view(kT, 1))
+        nc.sync.dma_start(out=raw["q", 1][:], in_=features_view(qT, 1))
+        for s in range(SETS):
+            nc.sync.dma_start(out=raw["v", s][:], in_=tokens_view(s))
         nc.scalar.activation(out=half_kb[:], in_=kb_sb[:], func=ACT.Copy, scale=0.5)
-        pack_k(0, 0, 64)
-        pack_k(0, 1, HEAD_SPLIT)
-        quantize("k", 0, 0, 256)
-        pack_q(0, 0, 0, 32)
-        pack_q(0, 0, 1, Q0_SPLIT)
-        quantize("k", 0, 256, 512)
-        quantize("q", 0, 0, 256)
-        pack_q(0, 1, 0, 32)
-        pack_q(0, 1, 1, 32)
+
+        pack_q(0, 0, 0, "vector")
+        pack_q(0, 0, 1, "scalar")
+        quantize("q", 0, 0, HALF)
+        pack_k(0, 0, "vector")
+        pack_k(0, 1, "scalar")
+        quantize("k", 0, 0, P)
+        quantize("k", 0, P, 2 * P)
+        pack_q(0, 1, 0, "vector")
+        pack_q(0, 1, 1, "vector", "scalar")
 
         last = H - 1
         issued = 0
-        base = 2 * EARLY
         for n in range(-1, steps + PRODUCT_LAG + STORE_LAG):
             if 0 <= n < steps:
                 cap(n)
-            if n == Q0B_STEP:
-                quantize("q", 0, 256, 512)
-            h = done_at.get(n - PRODUCT_LAG)
+            if n == 0:
+                quantize("k", 0, 2 * P, COLS)
+                quantize("q", 0, HALF, COLS)
+            h = ends_at.get(n - PRODUCT_LAG)
             if h is not None and h != last:
-                product(h, h % 2, 0, PACK)
-            while (
-                issued < min(steps, n + 4)
-                and all(bank_of(m) != bank_of(issued) for m in range(n + 1, issued))
-                and (issued < EARLY or n >= Q0B_STEP)
+                product(h, h % OUT_BANKS, 0, PACK)
+            while issued <= min(steps - 1, n + AHEAD) and all(
+                bank_of(m) != bank_of(issued) for m in range(n + 1, issued)
             ):
                 scores(issued)
                 issued = issued + 1
-            h = done_at.get(n - PRODUCT_LAG - STORE_LAG)
+            h = ends_at.get(n - PRODUCT_LAG - STORE_LAG)
             if h is not None and h != last:
-                store(h, h % 2, 0, PACK)
+                store(h, h % OUT_BANKS, 0, PACK, "scalar")
             if 0 <= n < steps:
                 weigh(n)
-            h = done_at.get(n - 1)
+            h = ends_at.get(n - 1)
             if h is not None:
-                if SHARE or h < SHARED_FROM:
-                    pack_w(h, "vector", 0, SHARE if h >= SHARED_FROM else P)
-            h = done_at.get(n - SHARE_LAG)
-            if h is not None and h >= SHARED_FROM and SHARE < P:
-                pack_w(h, "scalar", SHARE, P)
-            h = done_at.get(n - 2)
-            if h is not None and h < SHARED_FROM:
-                quantize_w(h, 0, NQ)
-            h = done_at.get(n - max(2, SHARE_LAG))
-            if h is not None and SHARED_FROM <= h < last:
-                quantize_w(h, 0, NQ)
-            h = done_at.get(n + V_LEAD)
+                pack_w(h)
+                pack_v(h, "vector" if h == 0 else "scalar")
+            h = ends_at.get(n - 2)
             if h is not None:
-                pack_v(h // PACK, h % PACK, "scalar" if VS_LO <= h < VS_HI else "vector")
-            h = done_at.get(n + V_LEAD - V_GAP)
-            if h is not None:
+                if h != last:
+                    quantize_w(h, 0, PACK)
                 quantize("v", h // PACK, P * (h % PACK), P * (h % PACK + 1))
-            if n == K1_STEP:
-                pack_k(1, 0, 64)
-                pack_k(1, 1, K1_SPLIT)
-            if n == K1_STEP + 1:
+            if n == K_STEP:
+                pack_k(1, 0, "vector")
+                pack_k(1, 1, "vector")
+            if n == K_STEP + 1:
                 quantize("k", 1)
-            if n == Q1_STEP:
-                pack_q(1, 0, 0, 32)
-                pack_q(1, 0, 1, Q1A_SPLIT)
-            if n == Q1_STEP + 1:
-                pack_q(1, 1, 0, Q1_SPLIT)
-                pack_q(1, 1, 1, 0)
-            if n == Q1_STEP + 2:
+            if n == Q_STEP:
+                pack_q(1, 0, 0, "vector")
+                pack_q(1, 0, 1, "vector")
+            if n == Q_STEP + 1:
+                pack_q(1, 1, 0, "vector", "scalar")
+                pack_q(1, 1, 1, "scalar")
+            if n == Q_STEP + 2:
                 quantize("q", 1)
-        for half in range(2):
-            quantize_w(last, 2 * P * half, 2 * P * (half + 1))
-            product(last, (last + half) % 2, 2 * half, 2 * half + 2)
-        store(last, last % 2, 0, 2)
-        store(last, (last + 1) % 2, 2, 4, LAST_ENGINE)
+
+        first_bank, second_bank = last % OUT_BANKS, (last + 1) % OUT_BANKS
+        quantize_w(last, 0, 2)
+        product(last, first_bank, 0, 2)
+        quantize_w(last, 2, PACK)
+        product(last, second_bank, 2, PACK)
+        store(last, first_bank, 0, 2, "scalar")
+        store(last, second_bank, 2, PACK, "vector")

from contextlib import ExitStack

import concourse.mybir as mybir

H, D, NQ, N = 8, 128, 512, 512
FLOPS = 2 * 2 * H * D * NQ * N

F32 = mybir.dt.float32
BF16 = mybir.dt.bfloat16
U32 = mybir.dt.uint32
U8 = mybir.dt.uint8
FP8X4 = mybir.dt.float8_e4m3fn_x4
ACT = mybir.ActivationFunctionType
ALU = mybir.AluOpType

P = 128
PACK = 4
ROWS = 32
SETS = H // PACK
COLS = 512
HALF = NQ // 2
OUT_SCALE = 2.0 / 16.0

SKEW = 3
SCORE_BANKS = (2, 1, 1, 2)
OUT_BANKS = 2
AHEAD = 3
EARLY_TILES = ((0, 0), (0, 1), (1, 0), (2, 0))
PRODUCT_LAG = 8
STORE_LAG = 3
K_STEP = 4
Q_STEP = 9


def tile_rows_a_relu_kb_cap_kernel(tc, qT, kT, t, v, kb, out):
    nc = tc.nc
    with ExitStack() as ctx:
        keep = ctx.enter_context(tc.tile_pool(name="keep", bufs=1))
        ring = ctx.enter_context(tc.tile_pool(name="ring", bufs=4))
        psum = ctx.enter_context(tc.psum_pool(name="psum", bufs=1))
        ctx.enter_context(tc.manual_schedule())

        def kept(name, shape, dtype):
            return keep.tile(shape, dtype, name=name, align_bytes=64)

        kb_sb = kept("kb_sb", [P, PACK], F32)
        t_sb = kept("t_sb", [P, PACK], F32)
        half_kb = kept("half_kb", [P, PACK], F32)
        raw, packed, codes, scales = {}, {}, {}, {}
        for name in ("k", "q", "v"):
            for s in range(SETS):
                if (name, s) == ("q", 0):
                    first_q = [kept("raw_q0%d" % u, [P, PACK, HALF], F32) for u in range(2)]
                else:
                    raw[name, s] = kept("raw_%s%d" % (name, s), [P, PACK, COLS], F32)
                packed[name, s] = kept("packed_%s%d" % (name, s), [P, COLS, PACK], BF16)
                codes[name, s] = kept("codes_%s%d" % (name, s), [P, COLS], U32)
                scales[name, s] = kept("scales_%s%d" % (name, s), [P, COLS], U8)
        score_banks = [
            [psum.tile([P, NQ], F32, name="score_%d_%d" % (g, b)) for b in range(SCORE_BANKS[g])] for g in range(PACK)
        ]
        out_banks = [psum.tile([P, NQ], F32, name="out_bank_%d" % b) for b in range(OUT_BANKS)]

        def features_view(x, s):
            return x[PACK * s : PACK * (s + 1)].rearrange("h (p j) n -> (h p) j n", j=PACK)

        def tokens_view(s):
            return v[PACK * s : PACK * (s + 1)].rearrange("h (p r) e -> p h (r e)", r=PACK)

        def half_cols(u):
            return slice(HALF * u, HALF * (u + 1))

        def copy_on(engine, dst, src):
            if engine == "vector":
                nc.vector.tensor_copy(out=dst, in_=src)
            else:
                nc.scalar.copy(out=dst, in_=src)

        def pack_dealt(dst, src, pair, engines):
            places = slice(2 * pair, 2 * pair + 2)
            dst = dst.rearrange("p (c a b) j -> p a j b c", c=PACK, b=2)[:, :, :, :, places]
            src = src.rearrange("p j (a b c) -> p a j b c", c=PACK, b=2)[:, :, :, :, places]
            share = dst.shape[1] // len(engines)
            for i, engine in enumerate(engines):
                copy_on(engine, dst[:, share * i : share * (i + 1)], src[:, share * i : share * (i + 1)])

        def pack_k(s, pair, *engines):
            pack_dealt(packed["k", s][:], raw["k", s][:], pair, engines)

        def pack_q(s, u, pair, *engines):
            src = first_q[u][:] if s == 0 else raw["q", s][:, :, half_cols(u)]
            pack_dealt(packed["q", s][:, half_cols(u), :], src, pair, engines)

        def pack_v(h, engine):
            s, g = divmod(h, PACK)
            dst = packed["v", s][:, P * g : P * (g + 1), :].rearrange("p (a i) r -> p a r i", i=PACK)
            src = raw["v", s][:, g, :].rearrange("p (r a i) -> p a r i", r=PACK, i=PACK)
            copy_on(engine, dst, src)

        def quantize(name, s, lo=0, hi=COLS):
            nc.vector.quantize_mx(
                out=codes[name, s][:, lo:hi].bitcast(FP8X4),
                scales=scales[name, s][:, lo:hi],
                in_=packed[name, s][:, lo:hi, :].rearrange("p n j -> p (n j)"),
            )

        tiles = sorted(((h, r) for h in range(H) for r in range(PACK)), key=lambda hr: PACK * hr[0] + SKEW * hr[1])
        order = [(h, r, u, u + 1) for u in range(2) for h, r in EARLY_TILES]
        order = order + [(h, r, 0, 2) for h, r in tiles if (h, r) not in EARLY_TILES]
        steps = len(order)
        ends_at = {order.index((h, PACK - 1, 0, 2)): h for h in range(H)}

        def bank_of(n):
            h, r, lo, hi = order[n]
            return h % PACK, r % SCORE_BANKS[h % PACK]

        def scores(n):
            h, r, lo, hi = order[n]
            s, g = divmod(h, PACK)
            rows = slice(ROWS * g, ROWS * (g + 1))
            tokens = slice(P * r, P * (r + 1))
            for block in range(2 * lo, 2 * hi):
                cols = slice(P * block, P * (block + 1))
                nc.tensor.matmul_mx(
                    out=score_banks[g][bank_of(n)[1]][:, cols],
                    lhsT=codes["k", s][rows, tokens].bitcast(FP8X4),
                    lhsT_scale=scales["k", s][rows, tokens],
                    rhs=codes["q", s][rows, cols].bitcast(FP8X4),
                    rhs_scale=scales["q", s][rows, cols],
                    start=True,
                    stop=True,
                )

        capped, paired, w_packed, w_codes, w_scales = {}, {}, {}, {}, {}

        def cap(n):
            h, r, lo, hi = order[n]
            g, b = bank_of(n)
            capped[n] = ring.tile([P, NQ], F32, name="capped", bufs=12)
            cols = slice(HALF * lo, HALF * hi)
            nc.scalar.activation(
                out=capped[n][:, cols],
                in_=score_banks[g][b][:, cols],
                func=ACT.Tanh,
                bias=half_kb[:, r : r + 1],
                scale=0.5,
            )

        def weigh(n):
            h, r, lo, hi = order[n]
            if h not in paired:
                paired[h] = ring.tile([P, 2, NQ, 2], BF16, name="paired", bufs=6)
            nc.vector.tensor_scalar(
                out=paired[h][:, r // 2, :, r % 2].rearrange("p (c u m) -> p u c m", c=PACK, u=2)[:, lo:hi],
                in0=capped[n][:].rearrange("p (u c m) -> p u c m", c=PACK, u=2)[:, lo:hi],
                scalar1=0.0,
                scalar2=t_sb[:, r : r + 1],
                op0=ALU.max,
                op1=ALU.mult,
            )

        def pack_w(h):
            w_packed[h] = ring.tile([P, NQ, PACK], BF16, name="w_packed", bufs=3, align_bytes=64)
            dst = w_packed[h][:].rearrange("p n r -> p (n r)").bitcast(F32)
            src = paired[h][:].rearrange("p x n y -> p (x n y)").bitcast(F32)
            nc.vector.tensor_copy(
                out=dst.rearrange("p (a i x) -> p a x i", i=2, x=2),
                in_=src.rearrange("p (x a i) -> p a x i", i=2, x=2),
            )

        def quantize_w(h, lo, hi):
            if h not in w_codes:
                w_codes[h] = ring.tile([P, NQ], U32, name="w_codes", align_bytes=64)
                w_scales[h] = ring.tile([P, NQ], U8, name="w_scales", align_bytes=64)
            cols = slice(P * lo, P * hi)
            nc.vector.quantize_mx(
                out=w_codes[h][:, cols].bitcast(FP8X4),
                scales=w_scales[h][:, cols],
                in_=w_packed[h][:, cols, :].rearrange("p n r -> p (n r)"),
            )

        def product(h, bank, lo, hi):
            s, g = divmod(h, PACK)
            feats = slice(P * g, P * (g + 1))
            for c in range(lo, hi):
                cols = slice(P * c, P * (c + 1))
                nc.tensor.matmul_mx(
                    out=out_banks[bank][:, cols],
                    lhsT=w_codes[h][:, cols].bitcast(FP8X4),
                    lhsT_scale=w_scales[h][:, cols],
                    rhs=codes["v", s][:, feats].bitcast(FP8X4),
                    rhs_scale=scales["v", s][:, feats],
                    start=True,
                    stop=True,
                )

        def store(h, bank, lo, hi, engine):
            cols = slice(P * lo, P * hi)
            result = ring.tile([P, NQ], F32, name="result", bufs=5)
            if engine == "scalar":
                nc.scalar.activation(out=result[:, cols], in_=out_banks[bank][:, cols], func=ACT.Copy, scale=OUT_SCALE)
            else:
                nc.vector.tensor_scalar(
                    out=result[:, cols], in0=out_banks[bank][:, cols], scalar1=OUT_SCALE, scalar2=None, op0=ALU.mult
                )
            nc.sync.dma_start(out=out[h].rearrange("(n c) e -> n (c e)", c=PACK)[:, cols], in_=result[:, cols])

        nc.scalar.dma_start(out=kb_sb[:], in_=kb.rearrange("(p r) o -> p (r o)", r=PACK))
        nc.scalar.dma_start(out=t_sb[:], in_=t.rearrange("(p r) o -> p (r o)", r=PACK))
        nc.sync.dma_start(out=first_q[0][:], in_=features_view(qT, 0)[:, :, half_cols(0)])
        nc.sync.dma_start(out=raw["k", 0][:], in_=features_view(kT, 0))
        nc.sync.dma_start(out=first_q[1][:], in_=features_view(qT, 0)[:, :, half_cols(1)])
        nc.sync.dma_start(out=raw["k", 1][:], in_=features_view(kT, 1))
        nc.sync.dma_start(out=raw["q", 1][:], in_=features_view(qT, 1))
        for s in range(SETS):
            nc.sync.dma_start(out=raw["v", s][:], in_=tokens_view(s))
        nc.scalar.activation(out=half_kb[:], in_=kb_sb[:], func=ACT.Copy, scale=0.5)

        pack_q(0, 0, 0, "vector")
        pack_q(0, 0, 1, "scalar")
        quantize("q", 0, 0, HALF)
        pack_k(0, 0, "vector")
        pack_k(0, 1, "scalar")
        quantize("k", 0, 0, P)
        quantize("k", 0, P, 2 * P)
        pack_q(0, 1, 0, "vector")
        pack_q(0, 1, 1, "vector", "scalar")

        last = H - 1
        issued = 0
        for n in range(-1, steps + PRODUCT_LAG + STORE_LAG):
            if 0 <= n < steps:
                cap(n)
            if n == 0:
                quantize("k", 0, 2 * P, COLS)
                quantize("q", 0, HALF, COLS)
            h = ends_at.get(n - PRODUCT_LAG)
            if h is not None and h != last:
                product(h, h % OUT_BANKS, 0, PACK)
            while issued <= min(steps - 1, n + AHEAD) and all(
                bank_of(m) != bank_of(issued) for m in range(n + 1, issued)
            ):
                scores(issued)
                issued = issued + 1
            h = ends_at.get(n - PRODUCT_LAG - STORE_LAG)
            if h is not None and h != last:
                store(h, h % OUT_BANKS, 0, PACK, "scalar")
            if 0 <= n < steps:
                weigh(n)
            h = ends_at.get(n - 1)
            if h is not None:
                pack_w(h)
                pack_v(h, "vector" if h == 0 else "scalar")
            h = ends_at.get(n - 2)
            if h is not None:
                if h != last:
                    quantize_w(h, 0, PACK)
                quantize("v", h // PACK, P * (h % PACK), P * (h % PACK + 1))
            if n == K_STEP:
                pack_k(1, 0, "vector")
                pack_k(1, 1, "vector")
            if n == K_STEP + 1:
                quantize("k", 1)
            if n == Q_STEP:
                pack_q(1, 0, 0, "vector")
                pack_q(1, 0, 1, "vector")
            if n == Q_STEP + 1:
                pack_q(1, 1, 0, "vector", "scalar")
                pack_q(1, 1, 1, "scalar")
            if n == Q_STEP + 2:
                quantize("q", 1)

        first_bank, second_bank = last % OUT_BANKS, (last + 1) % OUT_BANKS
        quantize_w(last, 0, 2)
        product(last, first_bank, 0, 2)
        quantize_w(last, 2, PACK)
        product(last, second_bank, 2, PACK)
        store(last, first_bank, 0, 2, "scalar")
        store(last, second_bank, 2, PACK, "vector")
